import numpy as np
import ml_dtypes


def mxq(x, axis, fmt="e4m3"):
    dtype, down = {"e4m3": (ml_dtypes.float8_e4m3fn, 7), "e5m2": (ml_dtypes.float8_e5m2, 14)}[fmt]
    v = np.moveaxis(np.asarray(x, np.float32).astype(ml_dtypes.bfloat16).astype(np.float64), axis, -1)
    blocks = v.reshape(v.shape[:-1] + (-1, 32))
    amax = np.abs(blocks).max(-1, keepdims=True)
    byte = np.maximum(np.where(amax > 0, np.frexp(amax)[1] - 1 + 127, 0) - down, 1)
    scale = np.exp2(byte - 127.0)
    codes = (blocks / scale).astype(np.float32).astype(dtype).astype(np.float64)
    return np.moveaxis((codes * scale).reshape(v.shape), -1, axis)


WIDE = False


def mx_kscale(k):
    if not WIDE:
        return np.ones(k)
    levels = np.array([10, -10, 5, -5, 0])
    if k % 512:
        return np.exp2(np.random.permutation(np.resize(levels, k // 32))).repeat(32)
    a = np.empty((k // 512, 16))
    for p in range(k // 512):
        a[p, :8] = np.random.permutation(np.resize(levels, 8))
        for g in range(8):
            far = levels[np.abs(levels - a[p, g]) >= 10]
            a[p, g + 8] = far[np.random.randint(len(far))]
    return np.exp2(a.ravel()).repeat(32)


def f64(x):
    return np.asarray(x).astype(np.float64)


def striped(idx):
    return np.tile(idx.reshape(-1, 16).T, (8, 1)).astype(np.uint16)


def unstriped(offs):
    return offs[:16].T.reshape(-1).astype(np.int64)


def striped8(idx):
    return np.concatenate([x.reshape(-1, 16).T for x in idx]).astype(np.uint16)


def runs(offs, k):
    lists = np.stack([offs[16 * r : 16 * r + 16].T.reshape(-1) for r in range(8)]).astype(np.int64)
    return lists[np.arange(k) % 512 // 64]


def pack_weight(w):
    k, n = w.shape
    w = f64(np.asarray(w, np.float32).astype(ml_dtypes.bfloat16)).reshape(k // 32, 32, n)
    amax = np.abs(w).max(1)
    byte = np.clip(np.where(amax > 0, np.frexp(amax)[1] - 1 + 127 - 7, 1), 1, 254)
    scaled = (w * np.exp2(127.0 - byte)[:, None, :]).reshape(k, n).astype(np.float32)
    words = np.ascontiguousarray(scaled.reshape(k // 512, 128, 4, n).transpose(0, 1, 3, 2)).astype(ml_dtypes.float8_e4m3fn).view(np.uint8)
    return words, np.ascontiguousarray(byte.astype(np.uint8).reshape(k // 512, 16, n))


def unpack_weight(words, scales):
    g, p, n, _ = words.shape
    vals = np.ascontiguousarray(words).view(ml_dtypes.float8_e4m3fn).astype(np.float64) * np.repeat(np.exp2(scales.astype(np.float64) - 127.0), 8, axis=1)[..., None]
    return vals.transpose(0, 1, 3, 2).reshape(g * 512, n)


def sigmoid(v):
    return 1.0 / (1.0 + np.exp(-np.maximum(v, -700.0)))


K, T, S, N, G, H, U = 512, 2048, 512, 512, 2048, 512, 1024


def setup_inputs():
    n = np.random.standard_normal
    s = mx_kscale(K)[:, None]
    u = mx_kscale(S)
    packed_xT = pack_weight(n((K, T)) * s)
    packed_dT = pack_weight(n((K, G)) / s)
    return {
        "x_words": packed_xT[0],
        "x_scales": packed_xT[1],
        "d_words": packed_dT[0],
        "d_scales": packed_dT[1],
        "gn": (np.random.uniform(0.5, 1.5, (H, 1)) * u[:, None]).astype(np.float32),
        "w1": (n((H, N)) / np.sqrt(H) / u[:, None]).astype(np.float32),
        "mem": n((N, U)).astype(np.float32),
        "offs": striped(np.random.permutation(T)[:S]),
        "kidx": striped8(np.random.randint(0, G, (8, H))),
        "n1": striped8(np.stack([np.random.permutation(S) for _ in range(8)])),
        "n2": striped8(np.stack([np.random.permutation(S) for _ in range(8)])),
        "n3": striped8(np.stack([np.random.permutation(U)[:S] for _ in range(8)])),
    }


def reference(x_words, x_scales, d_words, d_scales, gn, w1, mem, offs, kidx, n1, n2, n3):
    old = f64(mem)[np.arange(N)[:, None], runs(n3, N)]
    d_kidx = unpack_weight(d_words, d_scales)[np.arange(K)[:, None], runs(kidx, K)]
    xq = unpack_weight(x_words, x_scales)[:, unstriped(offs)]
    s = 0.0625 * (d_kidx.T @ xq)
    ex = np.exp(0.5 * s)
    z = f64(gn) * ((2.0 * ex) / (ex + ex[np.arange(H)[:, None], runs(n1, H)] + ex[np.arange(H)[:, None], runs(n2, H)]))
    h = mxq(f64(w1), 0, "e4m3").T @ mxq(z, 0, "e4m3")
    nw = old + sigmoid(h) * (h - old)
    out = f64(mem).copy()
    out[np.arange(N)[:, None], runs(n3, N)] = nw
    return out

@@ -1,0 +1,199 @@
+from contextlib import ExitStack
+
+import concourse.mybir as mybir
+
+FLOPS = 2 * 2 * 512 * 512 * 512
+
+F32 = mybir.dt.float32
+BF16 = mybir.dt.bfloat16
+I32 = mybir.dt.int32
+U32 = mybir.dt.uint32
+U16 = mybir.dt.uint16
+U8 = mybir.dt.uint8
+FP8X4 = mybir.dt.float8_e4m3fn_x4
+ACT = mybir.ActivationFunctionType
+ALU = mybir.AluOpType
+
+P = 128
+PACK = 4
+S = 512
+HALF = S // 2
+TABLE = 2048
+PAGE = 1024
+
+
+def tile_picked_keysharepaget_none_p_kernel(tc, x_words, x_scales, d_words, d_scales, gn, w1, mem, offs, kidx, n1, n2, n3, out):
+    nc = tc.nc
+    with ExitStack() as ctx:
+        keep = ctx.enter_context(tc.tile_pool(name="keep", bufs=1))
+        psum = ctx.enter_context(tc.psum_pool(name="psum", bufs=1))
+
+        def load_list(src, name):
+            tile = keep.tile([P, S // 16], U16, name=name)
+            nc.sync.dma_start(tile[:], src)
+            return tile
+
+        d_scale_table = keep.tile([P, TABLE], U8, name="d_scale_table", align_bytes=64)
+        x_scale_table = keep.tile([P, TABLE], U8, name="x_scale_table", tag="x_side", align_bytes=64)
+        nc.vector.memset(d_scale_table[:].bitcast(I32), 0)
+        nc.gpsimd.memset(x_scale_table[:].bitcast(I32), 0)
+
+        kidx_sb = load_list(kidx, "kidx_sb")
+        offs_sb = load_list(offs, "offs_sb")
+        d_word_table = keep.tile([P, TABLE], U32, name="d_word_table", tag="wide", align_bytes=64)
+        nc.sync.dma_start(d_word_table[:].bitcast(I32), d_words[0].rearrange("p n t -> p (n t)").bitcast(I32))
+        n1_sb = load_list(n1, "n1_sb")
+        n2_sb = load_list(n2, "n2_sb")
+        n3_sb = load_list(n3, "n3_sb")
+        x_word_table = keep.tile([P, TABLE], U32, name="x_word_table", align_bytes=64)
+        nc.sync.dma_start(x_word_table[:].bitcast(I32), x_words[0].rearrange("p n t -> p (n t)").bitcast(I32))
+        d_rows = d_scales[0].rearrange("(r j) c -> j r c", j=2)
+        for j in range(2):
+            nc.scalar.dma_start(d_scale_table[j:P:16, :].bitcast(I32), d_rows[j].bitcast(I32))
+        x_rows = x_scales[0].rearrange("(q i) c -> i q c", i=4)
+        for i in range(4):
+            queue = nc.gpsimd if i < 2 else nc.scalar
+            queue.dma_start(x_scale_table[i:P:32, :].bitcast(I32), x_rows[i].bitcast(I32))
+        gn_sb = keep.tile([P, PACK], F32, name="gn_sb")
+        nc.gpsimd.dma_start(gn_sb[:], gn.rearrange("(p t) o -> p (t o)", t=PACK))
+
+        ex = [keep.tile([P, PAGE], F32, name="ex%d" % t, tag="row%d" % t) for t in range(PACK)]
+        last_plain = keep.tile([P, S], F32, name="last_plain")
+        ex_plain = [ex[t + 1][:, S:] for t in range(PACK - 1)] + [last_plain[:]]
+        nc.vector.memset(ex[0][:, S:], 0.0)
+        warm = keep.tile([P, 8], F32, name="warm")
+        nc.scalar.activation(warm[:], ex[0][:, S : S + 8], ACT.Exp)
+
+        key_scales_picked = keep.tile([P, S], U8, name="key_scales_picked", tag="picked", align_bytes=64)
+        nc.vector.tensor_copy(key_scales_picked[:], d_scale_table[:].indirect(kidx_sb[:]))
+        key_scales = keep.tile([P, S], U8, name="key_scales", align_bytes=64)
+        nc.vector.tensor_copy(
+            key_scales[:].rearrange("p (t m) -> p m t", t=PACK),
+            key_scales_picked[:].rearrange("p (m t) -> p m t", t=PACK),
+        )
+        for j in range(2):
+            nc.scalar.dma_start(key_scales[2 + j : P : 32, :].bitcast(I32), key_scales[16 + j : P : 32, :].bitcast(I32))
+
+        key_words_picked = keep.tile([P, S], U32, name="key_words_picked", tag="picked", align_bytes=64)
+        nc.vector.tensor_copy(key_words_picked[:], d_word_table[:].indirect(kidx_sb[:]))
+        key_words = keep.tile([P, S], U32, name="key_words", align_bytes=64)
+        nc.vector.tensor_copy(
+            key_words[:].rearrange("p (t m) -> p m t", t=PACK),
+            key_words_picked[:].rearrange("p (m t) -> p m t", t=PACK),
+        )
+        query_scales = keep.tile([P, S], U8, name="query_scales", tag="picked", align_bytes=64)
+        nc.vector.tensor_copy(query_scales[:], x_scale_table[:].indirect(offs_sb[:]))
+        query_words = keep.tile([P, S], U32, name="query_words", tag="x_side", align_bytes=64)
+        nc.vector.tensor_copy(query_words[:], x_word_table[:].indirect(offs_sb[:]))
+
+        w_raw = keep.tile([P, PACK, S], F32, name="w_raw", tag="wide", align_bytes=64)
+        nc.sync.dma_start(w_raw[:], w1.rearrange("(p j) m -> p j m", j=PACK))
+
+        for t in range(PACK):
+            cols = slice(t * P, (t + 1) * P)
+            scores = psum.tile([P, S], F32, name="scores%d" % t)
+            nc.tensor.matmul_mx(
+                out=scores[:],
+                lhsT=key_words[:, cols].bitcast(FP8X4),
+                lhsT_scale=key_scales[:, cols],
+                rhs=query_words[:].bitcast(FP8X4),
+                rhs_scale=query_scales[:],
+                start=True,
+                stop=True,
+            )
+            nc.scalar.activation(ex[t][:, :S], scores[:], ACT.Exp, scale=0.03125)
+            nc.scalar.activation(ex_plain[t], scores[:], ACT.Exp, scale=0.03125)
+
+        w_words = keep.tile([P, S], U32, name="w_words", align_bytes=64)
+        w_scales = keep.tile([P, S], U8, name="w_scales", align_bytes=64)
+
+        def quantise_w(t):
+            cols = slice(t * P, (t + 1) * P)
+            w_grouped = keep.tile([P, P * PACK], BF16, name="w_grouped%d" % t, align_bytes=64)
+            nc.scalar.copy(
+                w_grouped[:].rearrange("p (b h l j) -> p b h j l", h=2, l=4, j=PACK),
+                w_raw[:].rearrange("p j (b t h l) -> p t b h j l", t=PACK, h=2, l=4)[:, t],
+            )
+            nc.vector.quantize_mx(out=w_words[:, cols].bitcast(FP8X4), scales=w_scales[:, cols], in_=w_grouped[:])
+
+        totals = []
+        for t in range(PACK):
+            part = keep.tile([P, S], F32, name="part%d" % t)
+            total = keep.tile([P, S], F32, name="total%d" % t)
+            nc.vector.tensor_tensor(part[:], ex[t][:].indirect(n1_sb[:]), ex_plain[t], ALU.add)
+            nc.vector.tensor_tensor(total[:], ex[t][:].indirect(n2_sb[:]), part[:], ALU.add)
+            totals.append(total)
+
+        z_rows = keep.tile([P, PACK, S], BF16, name="z_rows", align_bytes=64)
+        inverses = []
+        for t in range(PACK):
+            if t == PACK - 1:
+                quantise_w(0)
+            root = keep.tile([P, S], F32, name="root%d" % t)
+            inverse = keep.tile([P, S], F32, name="inverse%d" % t)
+            nc.scalar.activation(root[:], totals[t][:], ACT.Abs_reciprocal_sqrt, scale=0.5)
+            nc.scalar.activation(inverse[:], root[:], ACT.Square)
+            inverses.append(inverse)
+
+        def weigh(t, cols):
+            nc.vector.scalar_tensor_tensor(
+                z_rows[:, t, cols], ex_plain[t][:, cols], gn_sb[:, t : t + 1], inverses[t][:, cols], ALU.mult, ALU.mult
+            )
+
+        for t in range(PACK - 1):
+            weigh(t, slice(0, S))
+        warm_gate = keep.tile([P, 8], F32, name="warm_gate")
+        nc.scalar.activation(warm_gate[:], inverses[PACK - 1][:, :8], ACT.Silu)
+
+        z_words = []
+        z_scales = []
+        for u in range(2):
+            cols = slice(u * HALF, (u + 1) * HALF)
+            weigh(PACK - 1, cols)
+            z_grouped = keep.tile([P, HALF * PACK], BF16, name="z_grouped%d" % u, align_bytes=64)
+            nc.vector.tensor_copy(
+                z_grouped[:].rearrange("p (c i t) -> p c t i", i=4, t=PACK),
+                z_rows[:, :, cols].rearrange("p t (c i) -> p c t i", i=4),
+            )
+            words = keep.tile([P, HALF], U32, name="z_words%d" % u, align_bytes=64)
+            scales = keep.tile([P, HALF], U8, name="z_scales%d" % u, align_bytes=64)
+            nc.vector.quantize_mx(out=words[:].bitcast(FP8X4), scales=scales[:], in_=z_grouped[:])
+            z_words.append(words)
+            z_scales.append(scales)
+
+        mem_rows = mem.rearrange("(b t e) u -> t b e u", t=PACK, e=8)
+        out_rows = out.rearrange("(b t e) u -> t b e u", t=PACK, e=8)
+        for t in range(PACK):
+            if t + 1 < PACK:
+                quantise_w(t + 1)
+            page = keep.tile([P, PAGE], F32, name="page%d" % t, tag="row%d" % t)
+            nc.sync.dma_start(page[:], mem_rows[t])
+            rows = slice(t * P, (t + 1) * P)
+            pieces = [(0, HALF), (HALF, S)] if t == 0 else [(0, S)]
+            banks = []
+            for u in range(2):
+                if t == 0 or u == 0:
+                    h = psum.tile([P, S], F32, name="h%d_%d" % (t, u), tag="h%d" % ((t + u * 3) % 4))
+                banks.append(h)
+                nc.tensor.matmul_mx(
+                    out=h[:, u * HALF : (u + 1) * HALF],
+                    lhsT=w_words[:, rows].bitcast(FP8X4),
+                    lhsT_scale=w_scales[:, rows],
+                    rhs=z_words[u][:].bitcast(FP8X4),
+                    rhs_scale=z_scales[u][:],
+                    start=True,
+                    stop=True,
+                )
+            gated = keep.tile([P, S], F32, name="gated%d" % t)
+            half = keep.tile([P, S], F32, name="half%d" % t)
+            stay = keep.tile([P, S], F32, name="stay%d" % t)
+            kept = keep.tile([P, S], F32, name="kept%d" % t)
+            for u, (lo, hi) in enumerate(pieces):
+                cols = slice(lo, hi)
+                entries = n3_sb[:, lo // 16 : hi // 16]
+                nc.scalar.activation(half[:, cols], banks[u][:, cols], ACT.Tanh, scale=0.5)
+                nc.scalar.activation(stay[:, cols], half[:, cols], ACT.Copy, scale=-0.5, bias=0.5)
+                nc.scalar.activation(gated[:, cols], banks[u][:, cols], ACT.Silu)
+                nc.vector.tensor_tensor(kept[:, cols], page[:].indirect(entries), stay[:, cols], ALU.mult)
+                nc.vector.tensor_tensor(page[:].indirect(entries), kept[:, cols], gated[:, cols], ALU.add)
+            nc.sync.dma_start(out_rows[t], page[:])

@@ -33,102 +33,141 @@ def tile_picked_keysharepaget_none_p_kernel(tc, x_words, x_scales, d_words, d_sc
             nc.sync.dma_start(tile[:], src)
             return tile
 
-        d_scale_table = keep.tile([P, TABLE], U8, name="d_scale_table", align_bytes=64)
+        halves = [slice(0, HALF), slice(HALF, S)]
+
+        def entries(list_sb, cols):
+            return list_sb[:, cols.start // 16 : cols.stop // 16]
+
+        ex = [keep.tile([P, PAGE], F32, name="ex%d" % t, tag="row%d" % t) for t in range(PACK)]
+        ex_plain = [ex[t + 1][:, S:] for t in range(PACK - 1)] + [ex[PACK - 1][:, :S]]
+        last_scores = keep.tile([P, S], F32, name="last_scores")
+        last_first = keep.tile([P, S], F32, name="last_first")
+
+        zeros = keep.tile([P, 8], F32, name="zeros", tag="wide", align_bytes=64)
+        d_scale_table = keep.tile([P, TABLE], U8, name="d_scale_table", tag="d_side", align_bytes=64)
         x_scale_table = keep.tile([P, TABLE], U8, name="x_scale_table", tag="x_side", align_bytes=64)
+        warm_in = keep.tile([P, 8], F32, name="warm_in", tag="x_words", align_bytes=64)
+        warm_out = keep.tile([P, 8], F32, name="warm_out")
+        nc.vector.memset(zeros[:], 0.0)
+        nc.vector.memset(warm_in[:], 0.0)
         nc.vector.memset(d_scale_table[:].bitcast(I32), 0)
-        nc.gpsimd.memset(x_scale_table[:].bitcast(I32), 0)
+        nc.vector.tensor_copy(ex[0][:, S:], zeros[:, 0:1].to_broadcast([P, S]))
+        nc.vector.memset(x_scale_table[:].bitcast(I32), 0)
+        nc.scalar.activation(warm_out[:], warm_in[:], ACT.Exp)
 
         kidx_sb = load_list(kidx, "kidx_sb")
         offs_sb = load_list(offs, "offs_sb")
-        d_word_table = keep.tile([P, TABLE], U32, name="d_word_table", tag="wide", align_bytes=64)
-        nc.sync.dma_start(d_word_table[:].bitcast(I32), d_words[0].rearrange("p n t -> p (n t)").bitcast(I32))
         n1_sb = load_list(n1, "n1_sb")
         n2_sb = load_list(n2, "n2_sb")
         n3_sb = load_list(n3, "n3_sb")
-        x_word_table = keep.tile([P, TABLE], U32, name="x_word_table", align_bytes=64)
-        nc.sync.dma_start(x_word_table[:].bitcast(I32), x_words[0].rearrange("p n t -> p (n t)").bitcast(I32))
         d_rows = d_scales[0].rearrange("(r j) c -> j r c", j=2)
         for j in range(2):
-            nc.scalar.dma_start(d_scale_table[j:P:16, :].bitcast(I32), d_rows[j].bitcast(I32))
+            nc.sync.dma_start(d_scale_table[j:P:16, :].bitcast(I32), d_rows[j].bitcast(I32))
+        d_word_table = keep.tile([P, TABLE], U32, name="d_word_table", tag="wide", align_bytes=64)
+        nc.sync.dma_start(d_word_table[:].bitcast(I32), d_words[0].rearrange("p n t -> p (n t)").bitcast(I32))
         x_rows = x_scales[0].rearrange("(q i) c -> i q c", i=4)
         for i in range(4):
-            queue = nc.gpsimd if i < 2 else nc.scalar
-            queue.dma_start(x_scale_table[i:P:32, :].bitcast(I32), x_rows[i].bitcast(I32))
-        gn_sb = keep.tile([P, PACK], F32, name="gn_sb")
-        nc.gpsimd.dma_start(gn_sb[:], gn.rearrange("(p t) o -> p (t o)", t=PACK))
+            nc.sync.dma_start(x_scale_table[i:P:32, :].bitcast(I32), x_rows[i].bitcast(I32))
+        x_word_table = keep.tile([P, TABLE], U32, name="x_word_table", tag="x_words", align_bytes=64)
+        nc.sync.dma_start(x_word_table[:].bitcast(I32), x_words[0].rearrange("p n t -> p (n t)").bitcast(I32))
 
-        ex = [keep.tile([P, PAGE], F32, name="ex%d" % t, tag="row%d" % t) for t in range(PACK)]
-        last_plain = keep.tile([P, S], F32, name="last_plain")
-        ex_plain = [ex[t + 1][:, S:] for t in range(PACK - 1)] + [last_plain[:]]
-        nc.vector.memset(ex[0][:, S:], 0.0)
-        warm = keep.tile([P, 8], F32, name="warm")
-        nc.scalar.activation(warm[:], ex[0][:, S : S + 8], ACT.Exp)
-
-        key_scales_picked = keep.tile([P, S], U8, name="key_scales_picked", tag="picked", align_bytes=64)
+        key_scales_picked = keep.tile([P, S], U8, name="key_scales_picked", tag="early", align_bytes=64)
         nc.vector.tensor_copy(key_scales_picked[:], d_scale_table[:].indirect(kidx_sb[:]))
         key_scales = keep.tile([P, S], U8, name="key_scales", align_bytes=64)
         nc.vector.tensor_copy(
-            key_scales[:].rearrange("p (t m) -> p m t", t=PACK),
-            key_scales_picked[:].rearrange("p (m t) -> p m t", t=PACK),
+            key_scales[:].bitcast(I32).rearrange("p (t b e) -> p t b e", t=PACK, e=2),
+            key_scales_picked[:].bitcast(I32).rearrange("p (b t e) -> p t b e", t=PACK, e=2),
         )
         for j in range(2):
             nc.scalar.dma_start(key_scales[2 + j : P : 32, :].bitcast(I32), key_scales[16 + j : P : 32, :].bitcast(I32))
 
-        key_words_picked = keep.tile([P, S], U32, name="key_words_picked", tag="picked", align_bytes=64)
+        key_words_picked = keep.tile([P, S], U32, name="key_words_picked", tag="d_side", align_bytes=64)
         nc.vector.tensor_copy(key_words_picked[:], d_word_table[:].indirect(kidx_sb[:]))
+        query_scales = keep.tile([P, S], U8, name="query_scales", align_bytes=64)
+        nc.vector.tensor_copy(query_scales[:], x_scale_table[:].indirect(offs_sb[:]))
         key_words = keep.tile([P, S], U32, name="key_words", align_bytes=64)
         nc.vector.tensor_copy(
-            key_words[:].rearrange("p (t m) -> p m t", t=PACK),
-            key_words_picked[:].rearrange("p (m t) -> p m t", t=PACK),
+            key_words[:].rearrange("p (t b e) -> p t b e", t=PACK, e=8),
+            key_words_picked[:].rearrange("p (b t e) -> p t b e", t=PACK, e=8),
         )
-        query_scales = keep.tile([P, S], U8, name="query_scales", tag="picked", align_bytes=64)
-        nc.vector.tensor_copy(query_scales[:], x_scale_table[:].indirect(offs_sb[:]))
-        query_words = keep.tile([P, S], U32, name="query_words", tag="x_side", align_bytes=64)
-        nc.vector.tensor_copy(query_words[:], x_word_table[:].indirect(offs_sb[:]))
+        query_words = keep.tile([P, S], U32, name="query_words", align_bytes=64)
+        for cols in halves:
+            nc.vector.tensor_copy(query_words[:, cols], x_word_table[:].indirect(entries(offs_sb, cols)))
+
+        mem_rows = mem.rearrange("(b t e) u -> t b e u", t=PACK, e=8)
+        out_rows = out.rearrange("(b t e) u -> t b e u", t=PACK, e=8)
+        last_page = keep.tile([P, PAGE], F32, name="last_page", tag="early", align_bytes=64)
+        nc.sync.dma_start(last_page[:], mem_rows[PACK - 1])
+        last_old = keep.tile([P, S], F32, name="last_old")
+        nc.vector.tensor_copy(last_old[:], last_page[:].indirect(n3_sb[:]))
 
         w_raw = keep.tile([P, PACK, S], F32, name="w_raw", tag="wide", align_bytes=64)
-        nc.sync.dma_start(w_raw[:], w1.rearrange("(p j) m -> p j m", j=PACK))
+        w_rows = w1.rearrange("(b t e) m -> t b e m", t=PACK, e=8)
+        for t in range(PACK):
+            nc.sync.dma_start(w_raw[:, t, :], w_rows[t])
+        gn_sb = keep.tile([P, PACK, 8], F32, name="gn_sb", tag="x_side", align_bytes=64)
+        gn_rows = gn.rearrange("(b t e) o -> t b e o", t=PACK, e=8)
+        with nc.allow_non_contiguous_dma(reason="four single weights a partition"):
+            for t in range(PACK):
+                nc.sync.dma_start(gn_sb[:, t, 0:1], gn_rows[t])
 
         for t in range(PACK):
-            cols = slice(t * P, (t + 1) * P)
-            scores = psum.tile([P, S], F32, name="scores%d" % t)
-            nc.tensor.matmul_mx(
-                out=scores[:],
-                lhsT=key_words[:, cols].bitcast(FP8X4),
-                lhsT_scale=key_scales[:, cols],
-                rhs=query_words[:].bitcast(FP8X4),
-                rhs_scale=query_scales[:],
-                start=True,
-                stop=True,
-            )
-            nc.scalar.activation(ex[t][:, :S], scores[:], ACT.Exp, scale=0.03125)
-            nc.scalar.activation(ex_plain[t], scores[:], ACT.Exp, scale=0.03125)
+            rows = slice(t * P, (t + 1) * P)
+            for u, cols in enumerate(halves if t == 0 else [slice(0, S)]):
+                scores = psum.tile([P, S], F32, name="scores%d_%d" % (t, u), tag="bank%d" % (t + PACK * u))
+                nc.tensor.matmul_mx(
+                    out=scores[:, cols],
+                    lhsT=key_words[:, rows].bitcast(FP8X4),
+                    lhsT_scale=key_scales[:, rows],
+                    rhs=query_words[:, cols].bitcast(FP8X4),
+                    rhs_scale=query_scales[:, cols],
+                    start=True,
+                    stop=True,
+                )
+                if t == PACK - 1:
+                    nc.scalar.copy(last_scores[:], scores[:])
+                nc.scalar.activation(ex[t][:, cols], scores[:, cols], ACT.Exp, scale=0.03125)
+                if t < PACK - 1:
+                    nc.scalar.activation(ex_plain[t][:, cols], scores[:, cols], ACT.Exp, scale=0.03125)
+        for cols in halves:
+            nc.scalar.activation(last_first[:, cols], last_scores[:].indirect(entries(n1_sb, cols)), ACT.Exp, scale=0.03125)
 
         w_words = keep.tile([P, S], U32, name="w_words", align_bytes=64)
         w_scales = keep.tile([P, S], U8, name="w_scales", align_bytes=64)
 
-        def quantise_w(t):
-            cols = slice(t * P, (t + 1) * P)
-            w_grouped = keep.tile([P, P * PACK], BF16, name="w_grouped%d" % t, align_bytes=64)
-            nc.scalar.copy(
-                w_grouped[:].rearrange("p (b h l j) -> p b h j l", h=2, l=4, j=PACK),
-                w_raw[:].rearrange("p j (b t h l) -> p t b h j l", t=PACK, h=2, l=4)[:, t],
+        def quantise_w(first, count):
+            cols = slice(first * P, (first + count) * P)
+            w_grouped = keep.tile([P, count, P * PACK], BF16, name="w_grouped%d" % first, align_bytes=64)
+            for k in range(count):
+                nc.scalar.copy(
+                    w_grouped[:, k, :].rearrange("p (b h l j) -> p b h j l", h=2, l=4, j=PACK),
+                    w_raw[:].rearrange("p j (b t h l) -> p t b h j l", t=PACK, h=2, l=4)[:, first + k],
+                )
+            nc.vector.quantize_mx(
+                out=w_words[:, cols].bitcast(FP8X4), scales=w_scales[:, cols], in_=w_grouped[:].rearrange("p k c -> p (k c)")
             )
-            nc.vector.quantize_mx(out=w_words[:, cols].bitcast(FP8X4), scales=w_scales[:, cols], in_=w_grouped[:])
 
         totals = []
         for t in range(PACK):
             part = keep.tile([P, S], F32, name="part%d" % t)
             total = keep.tile([P, S], F32, name="total%d" % t)
-            nc.vector.tensor_tensor(part[:], ex[t][:].indirect(n1_sb[:]), ex_plain[t], ALU.add)
-            nc.vector.tensor_tensor(total[:], ex[t][:].indirect(n2_sb[:]), part[:], ALU.add)
+            if t < PACK - 1:
+                for cols in halves:
+                    nc.vector.tensor_tensor(part[:, cols], ex[t][:].indirect(entries(n1_sb, cols)), ex_plain[t][:, cols], ALU.add)
+                for cols in halves:
+                    nc.vector.tensor_tensor(total[:, cols], ex[t][:].indirect(entries(n2_sb, cols)), part[:, cols], ALU.add)
+            else:
+                for cols in halves:
+                    nc.vector.tensor_tensor(part[:, cols], ex[t][:].indirect(entries(n2_sb, cols)), last_first[:, cols], ALU.add)
+                for cols in halves:
+                    nc.vector.tensor_tensor(total[:, cols], part[:, cols], ex_plain[t][:, cols], ALU.add)
             totals.append(total)
 
         z_rows = keep.tile([P, PACK, S], BF16, name="z_rows", align_bytes=64)
         inverses = []
         for t in range(PACK):
             if t == PACK - 1:
-                quantise_w(0)
+                quantise_w(0, 1)
             root = keep.tile([P, S], F32, name="root%d" % t)
             inverse = keep.tile([P, S], F32, name="inverse%d" % t)
             nc.scalar.activation(root[:], totals[t][:], ACT.Abs_reciprocal_sqrt, scale=0.5)
@@ -137,7 +176,7 @@ def tile_picked_keysharepaget_none_p_kernel(tc, x_words, x_scales, d_words, d_sc
 
         def weigh(t, cols):
             nc.vector.scalar_tensor_tensor(
-                z_rows[:, t, cols], ex_plain[t][:, cols], gn_sb[:, t : t + 1], inverses[t][:, cols], ALU.mult, ALU.mult
+                z_rows[:, t, cols], ex_plain[t][:, cols], gn_sb[:, t, 0:1], inverses[t][:, cols], ALU.mult, ALU.mult
             )
 
         for t in range(PACK - 1):
@@ -145,11 +184,12 @@ def tile_picked_keysharepaget_none_p_kernel(tc, x_words, x_scales, d_words, d_sc
         warm_gate = keep.tile([P, 8], F32, name="warm_gate")
         nc.scalar.activation(warm_gate[:], inverses[PACK - 1][:, :8], ACT.Silu)
 
+        for cols in halves:
+            weigh(PACK - 1, cols)
+        quantise_w(1, 1)
         z_words = []
         z_scales = []
-        for u in range(2):
-            cols = slice(u * HALF, (u + 1) * HALF)
-            weigh(PACK - 1, cols)
+        for u, cols in enumerate(halves):
             z_grouped = keep.tile([P, HALF * PACK], BF16, name="z_grouped%d" % u, align_bytes=64)
             nc.vector.tensor_copy(
                 z_grouped[:].rearrange("p (c i t) -> p c t i", i=4, t=PACK),
@@ -161,39 +201,47 @@ def tile_picked_keysharepaget_none_p_kernel(tc, x_words, x_scales, d_words, d_sc
             z_words.append(words)
             z_scales.append(scales)
 
-        mem_rows = mem.rearrange("(b t e) u -> t b e u", t=PACK, e=8)
-        out_rows = out.rearrange("(b t e) u -> t b e u", t=PACK, e=8)
-        for t in range(PACK):
-            if t + 1 < PACK:
-                quantise_w(t + 1)
-            page = keep.tile([P, PAGE], F32, name="page%d" % t, tag="row%d" % t)
-            nc.sync.dma_start(page[:], mem_rows[t])
-            rows = slice(t * P, (t + 1) * P)
-            pieces = [(0, HALF), (HALF, S)] if t == 0 else [(0, S)]
-            banks = []
-            for u in range(2):
-                if t == 0 or u == 0:
-                    h = psum.tile([P, S], F32, name="h%d_%d" % (t, u), tag="h%d" % ((t + u * 3) % 4))
-                banks.append(h)
-                nc.tensor.matmul_mx(
-                    out=h[:, u * HALF : (u + 1) * HALF],
-                    lhsT=w_words[:, rows].bitcast(FP8X4),
-                    lhsT_scale=w_scales[:, rows],
-                    rhs=z_words[u][:].bitcast(FP8X4),
-                    rhs_scale=z_scales[u][:],
-                    start=True,
-                    stop=True,
-                )
-            gated = keep.tile([P, S], F32, name="gated%d" % t)
-            half = keep.tile([P, S], F32, name="half%d" % t)
-            stay = keep.tile([P, S], F32, name="stay%d" % t)
-            kept = keep.tile([P, S], F32, name="kept%d" % t)
-            for u, (lo, hi) in enumerate(pieces):
-                cols = slice(lo, hi)
-                entries = n3_sb[:, lo // 16 : hi // 16]
-                nc.scalar.activation(half[:, cols], banks[u][:, cols], ACT.Tanh, scale=0.5)
-                nc.scalar.activation(stay[:, cols], half[:, cols], ACT.Copy, scale=-0.5, bias=0.5)
-                nc.scalar.activation(gated[:, cols], banks[u][:, cols], ACT.Silu)
-                nc.vector.tensor_tensor(kept[:, cols], page[:].indirect(entries), stay[:, cols], ALU.mult)
-                nc.vector.tensor_tensor(page[:].indirect(entries), kept[:, cols], gated[:, cols], ALU.add)
-            nc.sync.dma_start(out_rows[t], page[:])
+        page = []
+        for t in range(PACK - 1):
+            tile = keep.tile([P, PAGE], F32, name="page%d" % t, tag="row%d" % t)
+            nc.sync.dma_start(tile[:], mem_rows[t])
+            page.append(tile)
+        page.append(last_page)
+
+        steps = [((0, 1), [0]), ((0, 1), [1]), ((2, 3), [0, 1])]
+        bank = PACK + 1
+        for step, (pair, parts) in enumerate(steps):
+            cols = slice(halves[parts[0]].start, halves[parts[-1]].stop)
+            width = cols.stop - cols.start
+            if step == 2:
+                quantise_w(2, 2)
+            h, stay, gated, kept = {}, {}, {}, {}
+            for t in pair:
+                rows = slice(t * P, (t + 1) * P)
+                h[t] = psum.tile([P, S], F32, name="h%d_%d" % (step, t), tag="bank%d" % (bank % 8))
+                bank = bank + 1
+                for k, u in enumerate(parts):
+                    nc.tensor.matmul_mx(
+                        out=h[t][:, k * HALF : (k + 1) * HALF],
+                        lhsT=w_words[:, rows].bitcast(FP8X4),
+                        lhsT_scale=w_scales[:, rows],
+                        rhs=z_words[u][:].bitcast(FP8X4),
+                        rhs_scale=z_scales[u][:],
+                        start=True,
+                        stop=True,
+                    )
+                half_gate = keep.tile([P, width], F32, name="half_gate%d_%d" % (step, t))
+                stay[t] = keep.tile([P, width], F32, name="stay%d_%d" % (step, t))
+                nc.scalar.activation(half_gate[:], h[t][:, :width], ACT.Tanh, scale=0.5)
+                nc.scalar.activation(stay[t][:], half_gate[:], ACT.Copy, scale=-0.5, bias=0.5)
+            for t in pair:
+                gated[t] = keep.tile([P, width], F32, name="gated%d_%d" % (step, t))
+                nc.scalar.activation(gated[t][:], h[t][:, :width], ACT.Silu)
+            for t in pair:
+                kept[t] = keep.tile([P, width], F32, name="kept%d_%d" % (step, t))
+                old = last_old[:] if t == PACK - 1 else page[t][:].indirect(entries(n3_sb, cols))
+                nc.vector.tensor_tensor(kept[t][:], old, stay[t][:], ALU.mult)
+            for t in pair:
+                nc.vector.tensor_tensor(page[t][:].indirect(entries(n3_sb, cols)), kept[t][:], gated[t][:], ALU.add)
+                if cols.stop == S:
+                    nc.sync.dma_start(out_rows[t], page[t][:])

from contextlib import ExitStack

import concourse.mybir as mybir

FLOPS = 2 * 2 * 512 * 512 * 512

F32 = mybir.dt.float32
BF16 = mybir.dt.bfloat16
I32 = mybir.dt.int32
U32 = mybir.dt.uint32
U16 = mybir.dt.uint16
U8 = mybir.dt.uint8
FP8X4 = mybir.dt.float8_e4m3fn_x4
ACT = mybir.ActivationFunctionType
ALU = mybir.AluOpType

P = 128
PACK = 4
S = 512
HALF = S // 2
TABLE = 2048
PAGE = 1024


def tile_picked_keysharepaget_none_p_kernel(tc, x_words, x_scales, d_words, d_scales, gn, w1, mem, offs, kidx, n1, n2, n3, out):
    nc = tc.nc
    with ExitStack() as ctx:
        keep = ctx.enter_context(tc.tile_pool(name="keep", bufs=1))
        psum = ctx.enter_context(tc.psum_pool(name="psum", bufs=1))

        def load_list(src, name):
            tile = keep.tile([P, S // 16], U16, name=name)
            nc.sync.dma_start(tile[:], src)
            return tile

        halves = [slice(0, HALF), slice(HALF, S)]

        def entries(list_sb, cols):
            return list_sb[:, cols.start // 16 : cols.stop // 16]

        ex = [keep.tile([P, PAGE], F32, name="ex%d" % t, tag="row%d" % t) for t in range(PACK)]
        ex_plain = [ex[t + 1][:, S:] for t in range(PACK - 1)] + [ex[PACK - 1][:, :S]]
        last_scores = keep.tile([P, S], F32, name="last_scores")
        last_first = keep.tile([P, S], F32, name="last_first")

        zeros = keep.tile([P, 8], F32, name="zeros", tag="wide", align_bytes=64)
        d_scale_table = keep.tile([P, TABLE], U8, name="d_scale_table", tag="d_side", align_bytes=64)
        x_scale_table = keep.tile([P, TABLE], U8, name="x_scale_table", tag="x_side", align_bytes=64)
        warm_in = keep.tile([P, 8], F32, name="warm_in", tag="x_words", align_bytes=64)
        warm_out = keep.tile([P, 8], F32, name="warm_out")
        nc.vector.memset(zeros[:], 0.0)
        nc.vector.memset(warm_in[:], 0.0)
        nc.vector.memset(d_scale_table[:].bitcast(I32), 0)
        nc.vector.tensor_copy(ex[0][:, S:], zeros[:, 0:1].to_broadcast([P, S]))
        nc.vector.memset(x_scale_table[:].bitcast(I32), 0)
        nc.scalar.activation(warm_out[:], warm_in[:], ACT.Exp)

        kidx_sb = load_list(kidx, "kidx_sb")
        offs_sb = load_list(offs, "offs_sb")
        n1_sb = load_list(n1, "n1_sb")
        n2_sb = load_list(n2, "n2_sb")
        n3_sb = load_list(n3, "n3_sb")
        d_rows = d_scales[0].rearrange("(r j) c -> j r c", j=2)
        for j in range(2):
            nc.sync.dma_start(d_scale_table[j:P:16, :].bitcast(I32), d_rows[j].bitcast(I32))
        d_word_table = keep.tile([P, TABLE], U32, name="d_word_table", tag="wide", align_bytes=64)
        nc.sync.dma_start(d_word_table[:].bitcast(I32), d_words[0].rearrange("p n t -> p (n t)").bitcast(I32))
        x_rows = x_scales[0].rearrange("(q i) c -> i q c", i=4)
        for i in range(4):
            nc.sync.dma_start(x_scale_table[i:P:32, :].bitcast(I32), x_rows[i].bitcast(I32))
        x_word_table = keep.tile([P, TABLE], U32, name="x_word_table", tag="x_words", align_bytes=64)
        nc.sync.dma_start(x_word_table[:].bitcast(I32), x_words[0].rearrange("p n t -> p (n t)").bitcast(I32))

        key_scales_picked = keep.tile([P, S], U8, name="key_scales_picked", tag="early", align_bytes=64)
        nc.vector.tensor_copy(key_scales_picked[:], d_scale_table[:].indirect(kidx_sb[:]))
        key_scales = keep.tile([P, S], U8, name="key_scales", align_bytes=64)
        nc.vector.tensor_copy(
            key_scales[:].bitcast(I32).rearrange("p (t b e) -> p t b e", t=PACK, e=2),
            key_scales_picked[:].bitcast(I32).rearrange("p (b t e) -> p t b e", t=PACK, e=2),
        )
        for j in range(2):
            nc.scalar.dma_start(key_scales[2 + j : P : 32, :].bitcast(I32), key_scales[16 + j : P : 32, :].bitcast(I32))

        key_words_picked = keep.tile([P, S], U32, name="key_words_picked", tag="d_side", align_bytes=64)
        nc.vector.tensor_copy(key_words_picked[:], d_word_table[:].indirect(kidx_sb[:]))
        query_scales = keep.tile([P, S], U8, name="query_scales", align_bytes=64)
        nc.vector.tensor_copy(query_scales[:], x_scale_table[:].indirect(offs_sb[:]))
        key_words = keep.tile([P, S], U32, name="key_words", align_bytes=64)
        nc.vector.tensor_copy(
            key_words[:].rearrange("p (t b e) -> p t b e", t=PACK, e=8),
            key_words_picked[:].rearrange("p (b t e) -> p t b e", t=PACK, e=8),
        )
        query_words = keep.tile([P, S], U32, name="query_words", align_bytes=64)
        for cols in halves:
            nc.vector.tensor_copy(query_words[:, cols], x_word_table[:].indirect(entries(offs_sb, cols)))

        mem_rows = mem.rearrange("(b t e) u -> t b e u", t=PACK, e=8)
        out_rows = out.rearrange("(b t e) u -> t b e u", t=PACK, e=8)
        last_page = keep.tile([P, PAGE], F32, name="last_page", tag="early", align_bytes=64)
        nc.sync.dma_start(last_page[:], mem_rows[PACK - 1])
        last_old = keep.tile([P, S], F32, name="last_old")
        nc.vector.tensor_copy(last_old[:], last_page[:].indirect(n3_sb[:]))

        w_raw = keep.tile([P, PACK, S], F32, name="w_raw", tag="wide", align_bytes=64)
        w_rows = w1.rearrange("(b t e) m -> t b e m", t=PACK, e=8)
        for t in range(PACK):
            nc.sync.dma_start(w_raw[:, t, :], w_rows[t])
        gn_sb = keep.tile([P, PACK, 8], F32, name="gn_sb", tag="x_side", align_bytes=64)
        gn_rows = gn.rearrange("(b t e) o -> t b e o", t=PACK, e=8)
        with nc.allow_non_contiguous_dma(reason="four single weights a partition"):
            for t in range(PACK):
                nc.sync.dma_start(gn_sb[:, t, 0:1], gn_rows[t])

        for t in range(PACK):
            rows = slice(t * P, (t + 1) * P)
            for u, cols in enumerate(halves if t == 0 else [slice(0, S)]):
                scores = psum.tile([P, S], F32, name="scores%d_%d" % (t, u), tag="bank%d" % (t + PACK * u))
                nc.tensor.matmul_mx(
                    out=scores[:, cols],
                    lhsT=key_words[:, rows].bitcast(FP8X4),
                    lhsT_scale=key_scales[:, rows],
                    rhs=query_words[:, cols].bitcast(FP8X4),
                    rhs_scale=query_scales[:, cols],
                    start=True,
                    stop=True,
                )
                if t == PACK - 1:
                    nc.scalar.copy(last_scores[:], scores[:])
                nc.scalar.activation(ex[t][:, cols], scores[:, cols], ACT.Exp, scale=0.03125)
                if t < PACK - 1:
                    nc.scalar.activation(ex_plain[t][:, cols], scores[:, cols], ACT.Exp, scale=0.03125)
        for cols in halves:
            nc.scalar.activation(last_first[:, cols], last_scores[:].indirect(entries(n1_sb, cols)), ACT.Exp, scale=0.03125)

        w_words = keep.tile([P, S], U32, name="w_words", align_bytes=64)
        w_scales = keep.tile([P, S], U8, name="w_scales", align_bytes=64)

        def quantise_w(first, count):
            cols = slice(first * P, (first + count) * P)
            w_grouped = keep.tile([P, count, P * PACK], BF16, name="w_grouped%d" % first, align_bytes=64)
            for k in range(count):
                nc.scalar.copy(
                    w_grouped[:, k, :].rearrange("p (b h l j) -> p b h j l", h=2, l=4, j=PACK),
                    w_raw[:].rearrange("p j (b t h l) -> p t b h j l", t=PACK, h=2, l=4)[:, first + k],
                )
            nc.vector.quantize_mx(
                out=w_words[:, cols].bitcast(FP8X4), scales=w_scales[:, cols], in_=w_grouped[:].rearrange("p k c -> p (k c)")
            )

        totals = []
        for t in range(PACK):
            part = keep.tile([P, S], F32, name="part%d" % t)
            total = keep.tile([P, S], F32, name="total%d" % t)
            if t < PACK - 1:
                for cols in halves:
                    nc.vector.tensor_tensor(part[:, cols], ex[t][:].indirect(entries(n1_sb, cols)), ex_plain[t][:, cols], ALU.add)
                for cols in halves:
                    nc.vector.tensor_tensor(total[:, cols], ex[t][:].indirect(entries(n2_sb, cols)), part[:, cols], ALU.add)
            else:
                for cols in halves:
                    nc.vector.tensor_tensor(part[:, cols], ex[t][:].indirect(entries(n2_sb, cols)), last_first[:, cols], ALU.add)
                for cols in halves:
                    nc.vector.tensor_tensor(total[:, cols], part[:, cols], ex_plain[t][:, cols], ALU.add)
            totals.append(total)

        z_rows = keep.tile([P, PACK, S], BF16, name="z_rows", align_bytes=64)
        inverses = []
        for t in range(PACK):
            if t == PACK - 1:
                quantise_w(0, 1)
            root = keep.tile([P, S], F32, name="root%d" % t)
            inverse = keep.tile([P, S], F32, name="inverse%d" % t)
            nc.scalar.activation(root[:], totals[t][:], ACT.Abs_reciprocal_sqrt, scale=0.5)
            nc.scalar.activation(inverse[:], root[:], ACT.Square)
            inverses.append(inverse)

        def weigh(t, cols):
            nc.vector.scalar_tensor_tensor(
                z_rows[:, t, cols], ex_plain[t][:, cols], gn_sb[:, t, 0:1], inverses[t][:, cols], ALU.mult, ALU.mult
            )

        for t in range(PACK - 1):
            weigh(t, slice(0, S))
        warm_gate = keep.tile([P, 8], F32, name="warm_gate")
        nc.scalar.activation(warm_gate[:], inverses[PACK - 1][:, :8], ACT.Silu)

        for cols in halves:
            weigh(PACK - 1, cols)
        quantise_w(1, 1)
        z_words = []
        z_scales = []
        for u, cols in enumerate(halves):
            z_grouped = keep.tile([P, HALF * PACK], BF16, name="z_grouped%d" % u, align_bytes=64)
            nc.vector.tensor_copy(
                z_grouped[:].rearrange("p (c i t) -> p c t i", i=4, t=PACK),
                z_rows[:, :, cols].rearrange("p t (c i) -> p c t i", i=4),
            )
            words = keep.tile([P, HALF], U32, name="z_words%d" % u, align_bytes=64)
            scales = keep.tile([P, HALF], U8, name="z_scales%d" % u, align_bytes=64)
            nc.vector.quantize_mx(out=words[:].bitcast(FP8X4), scales=scales[:], in_=z_grouped[:])
            z_words.append(words)
            z_scales.append(scales)

        page = []
        for t in range(PACK - 1):
            tile = keep.tile([P, PAGE], F32, name="page%d" % t, tag="row%d" % t)
            nc.sync.dma_start(tile[:], mem_rows[t])
            page.append(tile)
        page.append(last_page)

        steps = [((0, 1), [0]), ((0, 1), [1]), ((2, 3), [0, 1])]
        bank = PACK + 1
        for step, (pair, parts) in enumerate(steps):
            cols = slice(halves[parts[0]].start, halves[parts[-1]].stop)
            width = cols.stop - cols.start
            if step == 2:
                quantise_w(2, 2)
            h, stay, gated, kept = {}, {}, {}, {}
            for t in pair:
                rows = slice(t * P, (t + 1) * P)
                h[t] = psum.tile([P, S], F32, name="h%d_%d" % (step, t), tag="bank%d" % (bank % 8))
                bank = bank + 1
                for k, u in enumerate(parts):
                    nc.tensor.matmul_mx(
                        out=h[t][:, k * HALF : (k + 1) * HALF],
                        lhsT=w_words[:, rows].bitcast(FP8X4),
                        lhsT_scale=w_scales[:, rows],
                        rhs=z_words[u][:].bitcast(FP8X4),
                        rhs_scale=z_scales[u][:],
                        start=True,
                        stop=True,
                    )
                half_gate = keep.tile([P, width], F32, name="half_gate%d_%d" % (step, t))
                stay[t] = keep.tile([P, width], F32, name="stay%d_%d" % (step, t))
                nc.scalar.activation(half_gate[:], h[t][:, :width], ACT.Tanh, scale=0.5)
                nc.scalar.activation(stay[t][:], half_gate[:], ACT.Copy, scale=-0.5, bias=0.5)
            for t in pair:
                gated[t] = keep.tile([P, width], F32, name="gated%d_%d" % (step, t))
                nc.scalar.activation(gated[t][:], h[t][:, :width], ACT.Silu)
            for t in pair:
                kept[t] = keep.tile([P, width], F32, name="kept%d_%d" % (step, t))
                old = last_old[:] if t == PACK - 1 else page[t][:].indirect(entries(n3_sb, cols))
                nc.vector.tensor_tensor(kept[t][:], old, stay[t][:], ALU.mult)
            for t in pair:
                nc.vector.tensor_tensor(page[t][:].indirect(entries(n3_sb, cols)), kept[t][:], gated[t][:], ALU.add)
                if cols.stop == S:
                    nc.sync.dma_start(out_rows[t], page[t][:])
